import numpy as np
import ml_dtypes


def mxq(x, axis, fmt="e4m3"):
    dtype, down = {"e4m3": (ml_dtypes.float8_e4m3fn, 7), "e5m2": (ml_dtypes.float8_e5m2, 14)}[fmt]
    v = np.moveaxis(np.asarray(x, np.float32).astype(ml_dtypes.bfloat16).astype(np.float64), axis, -1)
    blocks = v.reshape(v.shape[:-1] + (-1, 32))
    amax = np.abs(blocks).max(-1, keepdims=True)
    byte = np.maximum(np.where(amax > 0, np.frexp(amax)[1] - 1 + 127, 0) - down, 1)
    scale = np.exp2(byte - 127.0)
    codes = (blocks / scale).astype(np.float32).astype(dtype).astype(np.float64)
    return np.moveaxis((codes * scale).reshape(v.shape), -1, axis)


WIDE = False


def mx_kscale(k):
    if not WIDE:
        return np.ones(k)
    levels = np.array([10, -10, 5, -5, 0])
    if k % 512:
        return np.exp2(np.random.permutation(np.resize(levels, k // 32))).repeat(32)
    a = np.empty((k // 512, 16))
    for p in range(k // 512):
        a[p, :8] = np.random.permutation(np.resize(levels, 8))
        for g in range(8):
            far = levels[np.abs(levels - a[p, g]) >= 10]
            a[p, g + 8] = far[np.random.randint(len(far))]
    return np.exp2(a.ravel()).repeat(32)


def f64(x):
    return np.asarray(x).astype(np.float64)


def striped(idx):
    return np.tile(idx.reshape(-1, 16).T, (8, 1)).astype(np.uint16)


def unstriped(offs):
    return offs[:16].T.reshape(-1).astype(np.int64)


def striped8(idx):
    return np.concatenate([x.reshape(-1, 16).T for x in idx]).astype(np.uint16)


def runs(offs, k):
    lists = np.stack([offs[16 * r : 16 * r + 16].T.reshape(-1) for r in range(8)]).astype(np.int64)
    return lists[np.arange(k) % 512 // 64]


def pack_weight(w):
    k, n = w.shape
    w = f64(np.asarray(w, np.float32).astype(ml_dtypes.bfloat16)).reshape(k // 32, 32, n)
    amax = np.abs(w).max(1)
    byte = np.clip(np.where(amax > 0, np.frexp(amax)[1] - 1 + 127 - 7, 1), 1, 254)
    scaled = (w * np.exp2(127.0 - byte)[:, None, :]).reshape(k, n).astype(np.float32)
    words = np.ascontiguousarray(scaled.reshape(k // 512, 128, 4, n).transpose(0, 1, 3, 2)).astype(ml_dtypes.float8_e4m3fn).view(np.uint8)
    return words, np.ascontiguousarray(byte.astype(np.uint8).reshape(k // 512, 16, n))


def unpack_weight(words, scales):
    g, p, n, _ = words.shape
    vals = np.ascontiguousarray(words).view(ml_dtypes.float8_e4m3fn).astype(np.float64) * np.repeat(np.exp2(scales.astype(np.float64) - 127.0), 8, axis=1)[..., None]
    return vals.transpose(0, 1, 3, 2).reshape(g * 512, n)


K, T, S, N, H = 512, 2048, 512, 512, 512


def setup_inputs():
    n = np.random.standard_normal
    s = mx_kscale(K)[:, None]
    u = mx_kscale(S)
    packed_xT = pack_weight(n((K, T)) * s)
    return {
        "x_words": packed_xT[0],
        "x_scales": packed_xT[1],
        "wa": (n((K, H)) / np.sqrt(K) / s).astype(np.float32),
        "wb": (n((K, H)) / np.sqrt(K) / s).astype(np.float32),
        "gt": (np.random.uniform(0.5, 1.5, (S, 1)) * u[:, None]).astype(np.float32),
        "w1": (n((S, N)) / np.sqrt(S) / u[:, None]).astype(np.float32),
        "offs": striped(np.random.permutation(T)[:S]),
        "two": striped(np.random.permutation(T)[:S]),
        "n1": striped8(np.stack([np.random.permutation(H) for _ in range(8)])),
        "n2": striped8(np.stack([np.random.permutation(H) for _ in range(8)])),
        "n3": striped8(np.stack([np.random.permutation(H) for _ in range(8)])),
    }


def reference(x_words, x_scales, wa, wb, gt, w1, offs, two, n1, n2, n3):
    xq = unpack_weight(x_words, x_scales)[:, unstriped(offs)]
    y = xq.T @ mxq(f64(wa), 0, "e4m3")
    x_two = unpack_weight(x_words, x_scales)[:, unstriped(two)]
    d = x_two.T @ mxq(f64(wb), 0, "e4m3")
    z = f64(gt) * (y * (np.tanh(d[np.arange(S)[:, None], runs(n1, S)] - (d[np.arange(S)[:, None], runs(n2, S)]))))
    h = mxq(f64(w1), 0, "e4m3").T @ mxq(z, 0, "e4m3")
    return h / (np.abs(h[np.arange(N)[:, None], runs(n3, N)]) + 0.5)

@@ -1,0 +1,234 @@
+from contextlib import ExitStack
+
+import concourse.mybir as mybir
+
+K, T, S, N, H = 512, 2048, 512, 512, 512
+FLOPS = 2 * K * S * H * 2 + 2 * S * N * H
+
+F32 = mybir.dt.float32
+BF16 = mybir.dt.bfloat16
+I32 = mybir.dt.int32
+U32 = mybir.dt.uint32
+U16 = mybir.dt.uint16
+U8 = mybir.dt.uint8
+FP8X4 = mybir.dt.float8_e4m3fn_x4
+ACT = mybir.ActivationFunctionType
+ALU = mybir.AluOpType
+
+P = 128
+PACK = 4
+HALF = H // 2
+LANE = 16
+
+
+def tile_picked_twtjointbnorm_none_p_kernel(
+    tc, x_words, x_scales, wa, wb, gt, w1, offs, two, n1, n2, n3, out
+):
+    nc = tc.nc
+    with ExitStack() as ctx:
+        lists = ctx.enter_context(tc.tile_pool(name="lists", bufs=1))
+        keep = ctx.enter_context(tc.tile_pool(name="keep", bufs=1))
+        psum = ctx.enter_context(tc.psum_pool(name="psum", bufs=1))
+
+        def sb(shape, dtype, name, tag=None):
+            return keep.tile(shape, dtype, name=name, tag=tag or name, align_bytes=64)
+
+        def load_list(src, name):
+            tile = lists.tile([P, S // LANE], U16, name=name)
+            nc.sync.dma_start(tile[:], src)
+            return tile
+
+        def halves(c):
+            return slice(c * HALF, (c + 1) * HALF)
+
+        def entries(lst, c):
+            return lst[:, c * HALF // LANE : (c + 1) * HALF // LANE]
+
+        words = sb([P, T], U32, "words")
+        planes = sb([P, T], U8, "planes")
+        shared = sb([P, PACK + 2, H], F32, "shared")
+        w1_raw = shared[:, 0:PACK, :]
+        bent = shared[:, 2 : PACK + 2, :]
+        nc.vector.memset(planes[:].bitcast(I32), 0)
+
+        def load_half(w, c, raw):
+            nc.sync.dma_start(raw, w.rearrange("(p j) n -> p j n", j=PACK)[:, :, halves(c)])
+            return raw
+
+        wb_raw = [load_half(wb, 0, sb([P, PACK, HALF], F32, "wb_raw0")[:])]
+        two_l = load_list(two, "two_l")
+        for q in range(4):
+            nc.sync.dma_start(
+                planes[32 * q : 32 * q + 4, :].bitcast(I32), x_scales[0, 4 * q : 4 * q + 4, :].bitcast(I32)
+            )
+        nc.sync.dma_start(words[:].bitcast(I32), x_words[0].rearrange("p n t -> p (n t)").bitcast(I32))
+        wb_raw.append(load_half(wb, 1, sb([P, PACK, HALF], F32, "wb_raw1")[:]))
+        offs_l = load_list(offs, "offs_l")
+        n2_l = load_list(n2, "n2_l")
+        n1_l = load_list(n1, "n1_l")
+        wa_raw = [load_half(wa, c, sb([P, PACK, HALF], F32, "wa_raw%d" % c)[:]) for c in range(2)]
+        gate = [bent[:, 2, 0:1], bent[:, 2, 8:9], bent[:, 3, 0:1], bent[:, 3, HALF : HALF + 1]]
+        with nc.allow_non_contiguous_dma(reason="one weight a partition"):
+            for t in range(PACK):
+                nc.gpsimd.dma_start(gate[t], gt.rearrange("(b t q) o -> t b q o", t=PACK, q=8)[t])
+        for t in range(PACK):
+            nc.sync.dma_start(w1_raw[:, t, :], w1.rearrange("(b t q) m -> t b q m", t=PACK, q=8)[t])
+        n3_l = load_list(n3, "n3_l")
+
+        def pick_scales(lst, name):
+            flat = sb([P, S], U8, name + "_flat")
+            nc.vector.tensor_copy(flat[:], planes[:].indirect(lst[:]))
+            scales = sb([P, S], U8, name + "_scales")
+            nc.vector.tensor_copy(
+                scales[:].bitcast(I32).rearrange("p (t b q) -> p b t q", t=PACK, q=2),
+                flat[:].bitcast(I32).rearrange("p (b t q) -> p b t q", t=PACK, q=2),
+            )
+            return scales
+
+        def pick_codes(lst, name, tag=None):
+            codes = sb([P, S], U32, name + "_codes", tag=tag)
+            nc.vector.tensor_copy(
+                codes[:].rearrange("p (t b q) -> p b t q", t=PACK, q=8), words[:].indirect(lst[:])
+            )
+            return codes
+
+        def weave(copy, raw, name):
+            width = raw.shape[2]
+            woven = sb([P, width, PACK], BF16, name)
+            copy(
+                woven[:].rearrange("p (a i) j -> p a j i", i=4),
+                raw.rearrange("p j (a i) -> p a j i", i=4),
+            )
+            return woven
+
+        def quantize(woven, name):
+            width = woven.shape[1]
+            codes = sb([P, width], U32, name + "_codes")
+            scales = sb([P, width], U8, name + "_scales")
+            nc.vector.quantize_mx(
+                out=codes[:].bitcast(FP8X4), scales=scales[:], in_=woven[:].rearrange("p n j -> p (n j)")
+            )
+            return codes, scales
+
+        def product(dst, stat, t, moving):
+            cols = slice(t * P, (t + 1) * P)
+            nc.tensor.matmul_mx(
+                out=dst,
+                lhsT=stat[0][:, cols].bitcast(FP8X4),
+                lhsT_scale=stat[1][:, cols],
+                rhs=moving[0][:].bitcast(FP8X4),
+                rhs_scale=moving[1][:],
+                start=True,
+                stop=True,
+            )
+
+        two_scales = pick_scales(two_l, "x_two")
+        wb_woven = [weave(nc.scalar.copy, wb_raw[c], "wb_woven%d" % c) for c in range(2)]
+        wb_q = [quantize(wb_woven[0], "wb0")]
+        x_two = pick_codes(two_l, "x_two"), two_scales
+        one_scales = pick_scales(offs_l, "x_one")
+        wb_q.append(quantize(wb_woven[1], "wb1"))
+        wa_woven = sb([P, H, PACK], BF16, "wa_woven")
+
+        def weave_wa(c):
+            nc.scalar.copy(
+                wa_woven[:, halves(c), :].rearrange("p (a i) j -> p a j i", i=4),
+                wa_raw[c].rearrange("p j (a i) -> p a j i", i=4),
+            )
+
+        d_sb = []
+        for t in range(PACK):
+            if t < 2:
+                weave_wa(t)
+            bank = psum.tile([P, H], F32, name="bank%d" % t)
+            for c in range(2):
+                product(bank[:, halves(c)], x_two, t, wb_q[c])
+            row = sb([P, H], F32, "d%d" % t)
+            nc.scalar.copy(row[:], bank[:])
+            d_sb.append(row)
+        x_one = pick_codes(offs_l, "x_one", tag="wb_woven1"), one_scales
+
+        diff = sb([P, PACK, H], F32, "diff")
+
+        def differ(t, low):
+            for c in range(2):
+                nc.vector.tensor_copy(low[:, halves(c)], d_sb[t][:].indirect(entries(n2_l, c)))
+            for c in range(2):
+                nc.vector.tensor_tensor(
+                    diff[:, t, halves(c)], d_sb[t][:].indirect(entries(n1_l, c)), low[:, halves(c)], ALU.subtract
+                )
+
+        differ(0, sb([P, H], F32, "low_first")[:])
+        wa_q = quantize(wa_woven, "wa")
+        lows = sb([P, PACK - 1, H], F32, "lows", tag="wa_woven")
+        w1_woven = sb([P, N, PACK], BF16, "w1_woven")
+        nc.scalar.copy(
+            w1_woven[:].rearrange("p (t m) j -> p m j t", t=PACK),
+            w1_raw.rearrange("p j (m t) -> p m j t", t=PACK),
+        )
+        nc.scalar.activation(bent[:, 0, :], diff[:, 0, :], ACT.Tanh)
+        differ(1, lows[:, 0, :])
+        nc.scalar.activation(bent[:, 1, :], diff[:, 1, :], ACT.Tanh)
+        yg = sb([P, PACK, H], F32, "yg")
+        for t in range(PACK):
+            bank = psum.tile([P, H], F32, name="bank%d" % (PACK + t))
+            product(bank[:], x_one, t, wa_q)
+            nc.scalar.activation(yg[:, t, :], bank[:], ACT.Copy, scale=gate[t])
+        differ(2, lows[:, 1, :])
+        nc.scalar.activation(bent[:, 2, :], diff[:, 2, :], ACT.Tanh)
+        differ(3, lows[:, 2, :])
+        w1_q = quantize(w1_woven, "w1")
+        for c in range(2):
+            nc.scalar.activation(bent[:, 3, halves(c)], diff[:, 3, halves(c)], ACT.Tanh)
+        nc.scalar.activation(diff[:, 3, H - 1 : H], d_sb[0][:, 0:1], ACT.Abs_reciprocal_sqrt, bias=0.5, scale=0.0)
+
+        z = []
+        for c in range(2):
+            zc = sb([P, HALF, PACK], BF16, "z%d" % c, tag="z")
+            nc.vector.tensor_tensor(
+                zc[:].rearrange("p (a i) t -> p a t i", i=4),
+                yg[:, :, halves(c)].rearrange("p t (a i) -> p a t i", i=4),
+                bent[:, :, halves(c)].rearrange("p t (a i) -> p a t i", i=4),
+                ALU.mult,
+            )
+            z.append(quantize(zc, "z%d" % c))
+        z_q = z
+
+        early = psum.tile([P, 2, HALF], F32, name="bank0")
+        late = [psum.tile([P, HALF], F32, name="bank%d" % (1 + t)) for t in range(2)]
+        whole = [psum.tile([P, 2, HALF], F32, name="bank%d" % (PACK + t)) for t in range(2)]
+        h = [[early[:, 0, :], late[0][:]], [early[:, 1, :], late[1][:]]] + [[w[:, 0, :], w[:, 1, :]] for w in whole]
+        for t, c in [(0, 0), (1, 0), (0, 1), (1, 1), (2, 0), (2, 1), (3, 0), (3, 1)]:
+            product(h[t][c], w1_q, t, z_q[c])
+
+        size = sb([P, PACK, H], F32, "size")
+        root = sb([P, PACK, H], F32, "root")
+        inv = [sb([P, H], F32, "inv%d" % t) for t in range(PACK)]
+        nc.scalar.activation(size[:, 0:2, halves(0)], early[:], ACT.Abs)
+        nc.scalar.activation(root[:, 0:2, halves(0)], size[:, 0:2, halves(0)], ACT.Abs_reciprocal_sqrt, bias=0.5)
+        for t in range(2):
+            nc.scalar.activation(inv[t][:, halves(0)], root[:, t, halves(0)], ACT.Square)
+        rows = out.rearrange("(p t) n -> p t n", t=PACK)
+        for t in range(PACK):
+            cols = halves(1) if t < 2 else slice(0, H)
+            src = late[t][:] if t < 2 else whole[t - 2][:].rearrange("p c n -> p (c n)")
+            nc.scalar.activation(size[:, t, cols], src, ACT.Abs)
+            if t == PACK - 1:
+                h_last = sb([P, H], F32, "h_last")
+                nc.scalar.copy(h_last[:], src)
+            nc.scalar.activation(root[:, t, cols], size[:, t, cols], ACT.Abs_reciprocal_sqrt, bias=0.5)
+            nc.scalar.activation(inv[t][:, cols], root[:, t, cols], ACT.Square)
+            res = sb([P, H], F32, "res%d" % t)
+            if t < PACK - 1:
+                got = sb([P, H], F32, "got%d" % t)
+                for c in range(2):
+                    nc.vector.tensor_copy(got[:, halves(c)], inv[t][:].indirect(entries(n3_l, c)))
+                for c in range(2):
+                    nc.vector.tensor_tensor(res[:, halves(c)], got[:, halves(c)], h[t][c], ALU.mult)
+                nc.sync.dma_start(rows[:, t, :], res[:])
+            else:
+                for c in range(2):
+                    nc.vector.tensor_tensor(
+                        res[:, halves(c)], inv[t][:].indirect(entries(n3_l, c)), h_last[:, halves(c)], ALU.mult
+                    )
+                    nc.sync.dma_start(rows[:, t, halves(c)], res[:, halves(c)])

@@ -1,6 +1,7 @@
 from contextlib import ExitStack
 
 import concourse.mybir as mybir
+from concourse.masks import make_identity
 
 K, T, S, N, H = 512, 2048, 512, 512, 512
 FLOPS = 2 * K * S * H * 2 + 2 * S * N * H
@@ -49,41 +50,44 @@ def tile_picked_twtjointbnorm_none_p_kernel(
         shared = sb([P, PACK + 2, H], F32, "shared")
         w1_raw = shared[:, 0:PACK, :]
         bent = shared[:, 2 : PACK + 2, :]
-        nc.vector.memset(planes[:].bitcast(I32), 0)
+        nc.vector.memset(planes[:, 0 : T // 2].bitcast(I32), 0)
+        nc.gpsimd.memset(planes[:, T // 2 : T].bitcast(I32), 0)
+        gate_rows = sb([P, P], F32, "gate_rows")
+        nc.gpsimd.memset(gate_rows[:], 0.0)
+        identity = sb([P, P], F32, "identity")
+        make_identity(nc, identity[:])
 
         def load_half(w, c, raw):
             nc.sync.dma_start(raw, w.rearrange("(p j) n -> p j n", j=PACK)[:, :, halves(c)])
             return raw
 
-        wb_raw = [load_half(wb, 0, sb([P, PACK, HALF], F32, "wb_raw0")[:])]
         two_l = load_list(two, "two_l")
+        offs_l = load_list(offs, "offs_l")
         for q in range(4):
             nc.sync.dma_start(
                 planes[32 * q : 32 * q + 4, :].bitcast(I32), x_scales[0, 4 * q : 4 * q + 4, :].bitcast(I32)
             )
         nc.sync.dma_start(words[:].bitcast(I32), x_words[0].rearrange("p n t -> p (n t)").bitcast(I32))
-        wb_raw.append(load_half(wb, 1, sb([P, PACK, HALF], F32, "wb_raw1")[:]))
-        offs_l = load_list(offs, "offs_l")
+        wb_raw = [load_half(wb, c, sb([P, PACK, HALF], F32, "wb_raw%d" % c)[:]) for c in range(2)]
         n2_l = load_list(n2, "n2_l")
         n1_l = load_list(n1, "n1_l")
         wa_raw = [load_half(wa, c, sb([P, PACK, HALF], F32, "wa_raw%d" % c)[:]) for c in range(2)]
-        gate = [bent[:, 2, 0:1], bent[:, 2, 8:9], bent[:, 3, 0:1], bent[:, 3, HALF : HALF + 1]]
-        with nc.allow_non_contiguous_dma(reason="one weight a partition"):
-            for t in range(PACK):
-                nc.gpsimd.dma_start(gate[t], gt.rearrange("(b t q) o -> t b q o", t=PACK, q=8)[t])
+        nc.sync.dma_start(
+            gate_rows[0:PACK, :].rearrange("t (b q) -> t b q", q=8),
+            gt.rearrange("(b t q) o -> t b (q o)", t=PACK, q=8),
+        )
         for t in range(PACK):
             nc.sync.dma_start(w1_raw[:, t, :], w1.rearrange("(b t q) m -> t b q m", t=PACK, q=8)[t])
         n3_l = load_list(n3, "n3_l")
 
-        def pick_scales(lst, name):
-            flat = sb([P, S], U8, name + "_flat")
-            nc.vector.tensor_copy(flat[:], planes[:].indirect(lst[:]))
-            scales = sb([P, S], U8, name + "_scales")
+        def pick_scales(lst, scales, first, last, name, tag=None):
+            count = last - first
+            flat = sb([P, count], U8, name, tag=tag)
+            nc.vector.tensor_copy(flat[:], planes[:].indirect(lst[:, first // LANE : last // LANE]))
             nc.vector.tensor_copy(
-                scales[:].bitcast(I32).rearrange("p (t b q) -> p b t q", t=PACK, q=2),
+                scales[:].bitcast(I32).rearrange("p (t b q) -> p b t q", t=PACK, q=2)[:, first // 32 : last // 32],
                 flat[:].bitcast(I32).rearrange("p (b t q) -> p b t q", t=PACK, q=2),
             )
-            return scales
 
         def pick_codes(lst, name, tag=None):
             codes = sb([P, S], U32, name + "_codes", tag=tag)
@@ -122,31 +126,39 @@ def tile_picked_twtjointbnorm_none_p_kernel(
                 stop=True,
             )
 
-        two_scales = pick_scales(two_l, "x_two")
-        wb_woven = [weave(nc.scalar.copy, wb_raw[c], "wb_woven%d" % c) for c in range(2)]
-        wb_q = [quantize(wb_woven[0], "wb0")]
+        two_scales = sb([P, S], U8, "two_scales")
+        one_scales = sb([P, S], U8, "one_scales")
+        pick_scales(two_l, two_scales, 0, S, "two_flat")
+        pick_scales(offs_l, one_scales, 0, S // 2, "one_flat0")
         x_two = pick_codes(two_l, "x_two"), two_scales
-        one_scales = pick_scales(offs_l, "x_one")
-        wb_q.append(quantize(wb_woven[1], "wb1"))
+        x_one = pick_codes(offs_l, "x_one"), one_scales
+        wb_q = [quantize(weave(nc.scalar.copy, wb_raw[c], "wb_woven%d" % c), "wb%d" % c) for c in range(2)]
+        pick_scales(offs_l, one_scales, S // 2, S, "one_flat1", tag="wb_woven1")
         wa_woven = sb([P, H, PACK], BF16, "wa_woven")
 
-        def weave_wa(c):
+        def weave_wa(c, cols):
             nc.scalar.copy(
-                wa_woven[:, halves(c), :].rearrange("p (a i) j -> p a j i", i=4),
-                wa_raw[c].rearrange("p j (a i) -> p a j i", i=4),
+                wa_woven[:, halves(c), :][:, cols, :].rearrange("p (a i) j -> p a j i", i=4),
+                wa_raw[c][:, :, cols].rearrange("p j (a i) -> p a j i", i=4),
             )
 
-        d_sb = []
-        for t in range(PACK):
-            if t < 2:
-                weave_wa(t)
+        d_sb = [sb([P, H], F32, "d%d" % t) for t in range(PACK)]
+        for c in range(2):
+            bank = psum.tile([P, HALF], F32, name="bank%d" % (PACK * c))
+            product(bank[:], x_two, 0, wb_q[c])
+            nc.scalar.copy(d_sb[0][:, halves(c)], bank[:])
+            weave_wa(0, slice(c * P, (c + 1) * P))
+        weave_wa(1, slice(0, HALF))
+        for t in range(1, PACK):
             bank = psum.tile([P, H], F32, name="bank%d" % t)
             for c in range(2):
                 product(bank[:, halves(c)], x_two, t, wb_q[c])
-            row = sb([P, H], F32, "d%d" % t)
-            nc.scalar.copy(row[:], bank[:])
-            d_sb.append(row)
-        x_one = pick_codes(offs_l, "x_one", tag="wb_woven1"), one_scales
+            nc.scalar.copy(d_sb[t][:], bank[:])
+
+        turned = psum.tile([P, P], F32, name="bank%d" % (2 * PACK - 1))
+        nc.tensor.transpose(turned[:], gate_rows[:], identity[:])
+        gate = bent[:, 2:4, :].rearrange("p u (c n) -> p (u c) n", n=HALF)[:, :, 0]
+        nc.scalar.copy(gate, turned[:, 0:PACK])
 
         diff = sb([P, PACK, H], F32, "diff")
 
@@ -173,7 +185,7 @@ def tile_picked_twtjointbnorm_none_p_kernel(
         for t in range(PACK):
             bank = psum.tile([P, H], F32, name="bank%d" % (PACK + t))
             product(bank[:], x_one, t, wa_q)
-            nc.scalar.activation(yg[:, t, :], bank[:], ACT.Copy, scale=gate[t])
+            nc.scalar.activation(yg[:, t, :], bank[:], ACT.Copy, scale=gate[:, t : t + 1])
         differ(2, lows[:, 1, :])
         nc.scalar.activation(bent[:, 2, :], diff[:, 2, :], ACT.Tanh)
         differ(3, lows[:, 2, :])
@@ -201,34 +213,44 @@ def tile_picked_twtjointbnorm_none_p_kernel(
         for t, c in [(0, 0), (1, 0), (0, 1), (1, 1), (2, 0), (2, 1), (3, 0), (3, 1)]:
             product(h[t][c], w1_q, t, z_q[c])
 
-        size = sb([P, PACK, H], F32, "size")
+        size = sb([P, 2, H], F32, "size")
         root = sb([P, PACK, H], F32, "root")
         inv = [sb([P, H], F32, "inv%d" % t) for t in range(PACK)]
-        nc.scalar.activation(size[:, 0:2, halves(0)], early[:], ACT.Abs)
-        nc.scalar.activation(root[:, 0:2, halves(0)], size[:, 0:2, halves(0)], ACT.Abs_reciprocal_sqrt, bias=0.5)
+        first, second = halves(0), halves(1)
+        nc.scalar.activation(size[:, :, first], early[:], ACT.Abs)
+        nc.scalar.activation(root[:, 0:2, first], size[:, :, first], ACT.Abs_reciprocal_sqrt, bias=0.5)
         for t in range(2):
-            nc.scalar.activation(inv[t][:, halves(0)], root[:, t, halves(0)], ACT.Square)
+            nc.vector.tensor_tensor(inv[t][:, first], root[:, t, first], root[:, t, first], ALU.mult)
+        for t in range(2):
+            nc.scalar.activation(size[:, t, second], late[t][:], ACT.Abs)
+        for t in range(2):
+            nc.scalar.activation(root[:, t, second], size[:, t, second], ACT.Abs_reciprocal_sqrt, bias=0.5)
+        for t in range(2):
+            nc.scalar.activation(inv[t][:, second], root[:, t, second], ACT.Square)
+        flat = [w[:].rearrange("p c n -> p (c n)") for w in whole]
+        for u in range(2):
+            nc.scalar.activation(size[:, u, :], flat[u], ACT.Abs)
+        h_sb = [root[:, u, :] for u in range(2)]
+        for u in range(2):
+            nc.scalar.activation(root[:, 2 + u, :], size[:, u, :], ACT.Abs_reciprocal_sqrt, bias=0.5)
+            nc.scalar.copy(h_sb[u], flat[u])
+            nc.scalar.activation(inv[2 + u][:], root[:, 2 + u, :], ACT.Square)
+
         rows = out.rearrange("(p t) n -> p t n", t=PACK)
         for t in range(PACK):
-            cols = halves(1) if t < 2 else slice(0, H)
-            src = late[t][:] if t < 2 else whole[t - 2][:].rearrange("p c n -> p (c n)")
-            nc.scalar.activation(size[:, t, cols], src, ACT.Abs)
-            if t == PACK - 1:
-                h_last = sb([P, H], F32, "h_last")
-                nc.scalar.copy(h_last[:], src)
-            nc.scalar.activation(root[:, t, cols], size[:, t, cols], ACT.Abs_reciprocal_sqrt, bias=0.5)
-            nc.scalar.activation(inv[t][:, cols], root[:, t, cols], ACT.Square)
             res = sb([P, H], F32, "res%d" % t)
-            if t < PACK - 1:
+            if t < 2:
                 got = sb([P, H], F32, "got%d" % t)
                 for c in range(2):
                     nc.vector.tensor_copy(got[:, halves(c)], inv[t][:].indirect(entries(n3_l, c)))
                 for c in range(2):
                     nc.vector.tensor_tensor(res[:, halves(c)], got[:, halves(c)], h[t][c], ALU.mult)
-                nc.sync.dma_start(rows[:, t, :], res[:])
             else:
                 for c in range(2):
                     nc.vector.tensor_tensor(
-                        res[:, halves(c)], inv[t][:].indirect(entries(n3_l, c)), h_last[:, halves(c)], ALU.mult
+                        res[:, halves(c)], inv[t][:].indirect(entries(n3_l, c)), h_sb[t - 2][:, halves(c)], ALU.mult
                     )
-                    nc.sync.dma_start(rows[:, t, halves(c)], res[:, halves(c)])
+                    if t == PACK - 1:
+                        nc.sync.dma_start(rows[:, t, halves(c)], res[:, halves(c)])
+            if t < PACK - 1:
+                nc.sync.dma_start(rows[:, t, :], res[:])

@@ -103,14 +103,14 @@ def tile_picked_twtjointbnorm_none_p_kernel(
                 woven[:].rearrange("p (a i) j -> p a j i", i=4),
                 raw.rearrange("p j (a i) -> p a j i", i=4),
             )
-            return woven
+            return woven[:]
 
-        def quantize(woven, name):
+        def quantize(woven, name, tag=None):
             width = woven.shape[1]
-            codes = sb([P, width], U32, name + "_codes")
+            codes = sb([P, width], U32, name + "_codes", tag=tag)
             scales = sb([P, width], U8, name + "_scales")
             nc.vector.quantize_mx(
-                out=codes[:].bitcast(FP8X4), scales=scales[:], in_=woven[:].rearrange("p n j -> p (n j)")
+                out=codes[:].bitcast(FP8X4), scales=scales[:], in_=woven.rearrange("p n j -> p (n j)")
             )
             return codes, scales
 
@@ -171,7 +171,7 @@ def tile_picked_twtjointbnorm_none_p_kernel(
                 )
 
         differ(0, sb([P, H], F32, "low_first")[:])
-        wa_q = quantize(wa_woven, "wa")
+        wa_q = quantize(wa_woven[:], "wa")
         lows = sb([P, PACK - 1, H], F32, "lows", tag="wa_woven")
         w1_woven = sb([P, N, PACK], BF16, "w1_woven")
         nc.scalar.copy(
@@ -189,45 +189,57 @@ def tile_picked_twtjointbnorm_none_p_kernel(
         differ(2, lows[:, 1, :])
         nc.scalar.activation(bent[:, 2, :], diff[:, 2, :], ACT.Tanh)
         differ(3, lows[:, 2, :])
-        w1_q = quantize(w1_woven, "w1")
+        w1_first = quantize(w1_woven[:, halves(0), :], "w1_first")
         for c in range(2):
             nc.scalar.activation(bent[:, 3, halves(c)], diff[:, 3, halves(c)], ACT.Tanh)
         nc.scalar.activation(diff[:, 3, H - 1 : H], d_sb[0][:, 0:1], ACT.Abs_reciprocal_sqrt, bias=0.5, scale=0.0)
 
-        z = []
-        for c in range(2):
-            zc = sb([P, HALF, PACK], BF16, "z%d" % c, tag="z")
+        def quarter(u):
+            return slice(u * P, (u + 1) * P)
+
+        def mix(u):
+            zu = sb([P, P, PACK], BF16, "z%d" % u)
             nc.vector.tensor_tensor(
-                zc[:].rearrange("p (a i) t -> p a t i", i=4),
-                yg[:, :, halves(c)].rearrange("p t (a i) -> p a t i", i=4),
-                bent[:, :, halves(c)].rearrange("p t (a i) -> p a t i", i=4),
+                zu[:].rearrange("p (a i) t -> p a t i", i=4),
+                yg[:, :, quarter(u)].rearrange("p t (a i) -> p a t i", i=4),
+                bent[:, :, quarter(u)].rearrange("p t (a i) -> p a t i", i=4),
                 ALU.mult,
             )
-            z.append(quantize(zc, "z%d" % c))
-        z_q = z
+            return zu[:]
 
-        early = psum.tile([P, 2, HALF], F32, name="bank0")
-        late = [psum.tile([P, HALF], F32, name="bank%d" % (1 + t)) for t in range(2)]
-        whole = [psum.tile([P, 2, HALF], F32, name="bank%d" % (PACK + t)) for t in range(2)]
-        h = [[early[:, 0, :], late[0][:]], [early[:, 1, :], late[1][:]]] + [[w[:, 0, :], w[:, 1, :]] for w in whole]
-        for t, c in [(0, 0), (1, 0), (0, 1), (1, 1), (2, 0), (2, 1), (3, 0), (3, 1)]:
-            product(h[t][c], w1_q, t, z_q[c])
+        z = [mix(0)]
+        z_q = []
+        for u in range(PACK):
+            if u + 1 < PACK:
+                z.append(mix(u + 1))
+            z_q.append(quantize(z[u], "z%d" % u))
+        w1_second = quantize(w1_woven[:, halves(1), :], "w1_second", tag="z0")
 
+        pair = [psum.tile([P, 2, P], F32, name="bank%d" % u) for u in range(PACK)]
+        whole = [psum.tile([P, H], F32, name="bank%d" % (PACK + e)) for e in range(2)]
         size = sb([P, 2, H], F32, "size")
         root = sb([P, PACK, H], F32, "root")
         inv = [sb([P, H], F32, "inv%d" % t) for t in range(PACK)]
-        first, second = halves(0), halves(1)
-        nc.scalar.activation(size[:, :, first], early[:], ACT.Abs)
-        nc.scalar.activation(root[:, 0:2, first], size[:, :, first], ACT.Abs_reciprocal_sqrt, bias=0.5)
+
+        def invert_root(u):
+            nc.scalar.activation(root[:, 0:2, quarter(u)], size[:, :, quarter(u)], ACT.Abs_reciprocal_sqrt, bias=0.5)
+
+        for u in range(PACK):
+            for t in range(2):
+                product(pair[u][:, t, :], w1_first, t, z_q[u])
+            nc.scalar.activation(size[:, :, quarter(u)], pair[u][:], ACT.Abs)
+            if u > 0:
+                invert_root(u - 1)
+        invert_root(PACK - 1)
+        for e in range(2):
+            for u in range(PACK):
+                product(whole[e][:, quarter(u)], w1_second, e, z_q[u])
+        for cols in (halves(0), quarter(2)):
+            for t in range(2):
+                nc.vector.tensor_tensor(inv[t][:, cols], root[:, t, cols], root[:, t, cols], ALU.mult)
         for t in range(2):
-            nc.vector.tensor_tensor(inv[t][:, first], root[:, t, first], root[:, t, first], ALU.mult)
-        for t in range(2):
-            nc.scalar.activation(size[:, t, second], late[t][:], ACT.Abs)
-        for t in range(2):
-            nc.scalar.activation(root[:, t, second], size[:, t, second], ACT.Abs_reciprocal_sqrt, bias=0.5)
-        for t in range(2):
-            nc.scalar.activation(inv[t][:, second], root[:, t, second], ACT.Square)
-        flat = [w[:].rearrange("p c n -> p (c n)") for w in whole]
+            nc.scalar.activation(inv[t][:, quarter(3)], root[:, t, quarter(3)], ACT.Square)
+        flat = [w[:] for w in whole]
         for u in range(2):
             nc.scalar.activation(size[:, u, :], flat[u], ACT.Abs)
         h_sb = [root[:, u, :] for u in range(2)]
@@ -243,8 +255,8 @@ def tile_picked_twtjointbnorm_none_p_kernel(
                 got = sb([P, H], F32, "got%d" % t)
                 for c in range(2):
                     nc.vector.tensor_copy(got[:, halves(c)], inv[t][:].indirect(entries(n3_l, c)))
-                for c in range(2):
-                    nc.vector.tensor_tensor(res[:, halves(c)], got[:, halves(c)], h[t][c], ALU.mult)
+                for u in range(PACK):
+                    nc.vector.tensor_tensor(res[:, quarter(u)], got[:, quarter(u)], pair[u][:, t, :], ALU.mult)
             else:
                 for c in range(2):
                     nc.vector.tensor_tensor(

from contextlib import ExitStack

import concourse.mybir as mybir
from concourse.masks import make_identity

K, T, S, N, H = 512, 2048, 512, 512, 512
FLOPS = 2 * K * S * H * 2 + 2 * S * N * H

F32 = mybir.dt.float32
BF16 = mybir.dt.bfloat16
I32 = mybir.dt.int32
U32 = mybir.dt.uint32
U16 = mybir.dt.uint16
U8 = mybir.dt.uint8
FP8X4 = mybir.dt.float8_e4m3fn_x4
ACT = mybir.ActivationFunctionType
ALU = mybir.AluOpType

P = 128
PACK = 4
HALF = H // 2
LANE = 16


def tile_picked_twtjointbnorm_none_p_kernel(
    tc, x_words, x_scales, wa, wb, gt, w1, offs, two, n1, n2, n3, out
):
    nc = tc.nc
    with ExitStack() as ctx:
        lists = ctx.enter_context(tc.tile_pool(name="lists", bufs=1))
        keep = ctx.enter_context(tc.tile_pool(name="keep", bufs=1))
        psum = ctx.enter_context(tc.psum_pool(name="psum", bufs=1))

        def sb(shape, dtype, name, tag=None):
            return keep.tile(shape, dtype, name=name, tag=tag or name, align_bytes=64)

        def load_list(src, name):
            tile = lists.tile([P, S // LANE], U16, name=name)
            nc.sync.dma_start(tile[:], src)
            return tile

        def halves(c):
            return slice(c * HALF, (c + 1) * HALF)

        def entries(lst, c):
            return lst[:, c * HALF // LANE : (c + 1) * HALF // LANE]

        words = sb([P, T], U32, "words")
        planes = sb([P, T], U8, "planes")
        shared = sb([P, PACK + 2, H], F32, "shared")
        w1_raw = shared[:, 0:PACK, :]
        bent = shared[:, 2 : PACK + 2, :]
        nc.vector.memset(planes[:, 0 : T // 2].bitcast(I32), 0)
        nc.gpsimd.memset(planes[:, T // 2 : T].bitcast(I32), 0)
        gate_rows = sb([P, P], F32, "gate_rows")
        nc.gpsimd.memset(gate_rows[:], 0.0)
        identity = sb([P, P], F32, "identity")
        make_identity(nc, identity[:])

        def load_half(w, c, raw):
            nc.sync.dma_start(raw, w.rearrange("(p j) n -> p j n", j=PACK)[:, :, halves(c)])
            return raw

        two_l = load_list(two, "two_l")
        offs_l = load_list(offs, "offs_l")
        for q in range(4):
            nc.sync.dma_start(
                planes[32 * q : 32 * q + 4, :].bitcast(I32), x_scales[0, 4 * q : 4 * q + 4, :].bitcast(I32)
            )
        nc.sync.dma_start(words[:].bitcast(I32), x_words[0].rearrange("p n t -> p (n t)").bitcast(I32))
        wb_raw = [load_half(wb, c, sb([P, PACK, HALF], F32, "wb_raw%d" % c)[:]) for c in range(2)]
        n2_l = load_list(n2, "n2_l")
        n1_l = load_list(n1, "n1_l")
        wa_raw = [load_half(wa, c, sb([P, PACK, HALF], F32, "wa_raw%d" % c)[:]) for c in range(2)]
        nc.sync.dma_start(
            gate_rows[0:PACK, :].rearrange("t (b q) -> t b q", q=8),
            gt.rearrange("(b t q) o -> t b (q o)", t=PACK, q=8),
        )
        for t in range(PACK):
            nc.sync.dma_start(w1_raw[:, t, :], w1.rearrange("(b t q) m -> t b q m", t=PACK, q=8)[t])
        n3_l = load_list(n3, "n3_l")

        def pick_scales(lst, scales, first, last, name, tag=None):
            count = last - first
            flat = sb([P, count], U8, name, tag=tag)
            nc.vector.tensor_copy(flat[:], planes[:].indirect(lst[:, first // LANE : last // LANE]))
            nc.vector.tensor_copy(
                scales[:].bitcast(I32).rearrange("p (t b q) -> p b t q", t=PACK, q=2)[:, first // 32 : last // 32],
                flat[:].bitcast(I32).rearrange("p (b t q) -> p b t q", t=PACK, q=2),
            )

        def pick_codes(lst, name, tag=None):
            codes = sb([P, S], U32, name + "_codes", tag=tag)
            nc.vector.tensor_copy(
                codes[:].rearrange("p (t b q) -> p b t q", t=PACK, q=8), words[:].indirect(lst[:])
            )
            return codes

        def weave(copy, raw, name):
            width = raw.shape[2]
            woven = sb([P, width, PACK], BF16, name)
            copy(
                woven[:].rearrange("p (a i) j -> p a j i", i=4),
                raw.rearrange("p j (a i) -> p a j i", i=4),
            )
            return woven[:]

        def quantize(woven, name, tag=None):
            width = woven.shape[1]
            codes = sb([P, width], U32, name + "_codes", tag=tag)
            scales = sb([P, width], U8, name + "_scales")
            nc.vector.quantize_mx(
                out=codes[:].bitcast(FP8X4), scales=scales[:], in_=woven.rearrange("p n j -> p (n j)")
            )
            return codes, scales

        def product(dst, stat, t, moving):
            cols = slice(t * P, (t + 1) * P)
            nc.tensor.matmul_mx(
                out=dst,
                lhsT=stat[0][:, cols].bitcast(FP8X4),
                lhsT_scale=stat[1][:, cols],
                rhs=moving[0][:].bitcast(FP8X4),
                rhs_scale=moving[1][:],
                start=True,
                stop=True,
            )

        two_scales = sb([P, S], U8, "two_scales")
        one_scales = sb([P, S], U8, "one_scales")
        pick_scales(two_l, two_scales, 0, S, "two_flat")
        pick_scales(offs_l, one_scales, 0, S // 2, "one_flat0")
        x_two = pick_codes(two_l, "x_two"), two_scales
        x_one = pick_codes(offs_l, "x_one"), one_scales
        wb_q = [quantize(weave(nc.scalar.copy, wb_raw[c], "wb_woven%d" % c), "wb%d" % c) for c in range(2)]
        pick_scales(offs_l, one_scales, S // 2, S, "one_flat1", tag="wb_woven1")
        wa_woven = sb([P, H, PACK], BF16, "wa_woven")

        def weave_wa(c, cols):
            nc.scalar.copy(
                wa_woven[:, halves(c), :][:, cols, :].rearrange("p (a i) j -> p a j i", i=4),
                wa_raw[c][:, :, cols].rearrange("p j (a i) -> p a j i", i=4),
            )

        d_sb = [sb([P, H], F32, "d%d" % t) for t in range(PACK)]
        for c in range(2):
            bank = psum.tile([P, HALF], F32, name="bank%d" % (PACK * c))
            product(bank[:], x_two, 0, wb_q[c])
            nc.scalar.copy(d_sb[0][:, halves(c)], bank[:])
            weave_wa(0, slice(c * P, (c + 1) * P))
        weave_wa(1, slice(0, HALF))
        for t in range(1, PACK):
            bank = psum.tile([P, H], F32, name="bank%d" % t)
            for c in range(2):
                product(bank[:, halves(c)], x_two, t, wb_q[c])
            nc.scalar.copy(d_sb[t][:], bank[:])

        turned = psum.tile([P, P], F32, name="bank%d" % (2 * PACK - 1))
        nc.tensor.transpose(turned[:], gate_rows[:], identity[:])
        gate = bent[:, 2:4, :].rearrange("p u (c n) -> p (u c) n", n=HALF)[:, :, 0]
        nc.scalar.copy(gate, turned[:, 0:PACK])

        diff = sb([P, PACK, H], F32, "diff")

        def differ(t, low):
            for c in range(2):
                nc.vector.tensor_copy(low[:, halves(c)], d_sb[t][:].indirect(entries(n2_l, c)))
            for c in range(2):
                nc.vector.tensor_tensor(
                    diff[:, t, halves(c)], d_sb[t][:].indirect(entries(n1_l, c)), low[:, halves(c)], ALU.subtract
                )

        differ(0, sb([P, H], F32, "low_first")[:])
        wa_q = quantize(wa_woven[:], "wa")
        lows = sb([P, PACK - 1, H], F32, "lows", tag="wa_woven")
        w1_woven = sb([P, N, PACK], BF16, "w1_woven")
        nc.scalar.copy(
            w1_woven[:].rearrange("p (t m) j -> p m j t", t=PACK),
            w1_raw.rearrange("p j (m t) -> p m j t", t=PACK),
        )
        nc.scalar.activation(bent[:, 0, :], diff[:, 0, :], ACT.Tanh)
        differ(1, lows[:, 0, :])
        nc.scalar.activation(bent[:, 1, :], diff[:, 1, :], ACT.Tanh)
        yg = sb([P, PACK, H], F32, "yg")
        for t in range(PACK):
            bank = psum.tile([P, H], F32, name="bank%d" % (PACK + t))
            product(bank[:], x_one, t, wa_q)
            nc.scalar.activation(yg[:, t, :], bank[:], ACT.Copy, scale=gate[:, t : t + 1])
        differ(2, lows[:, 1, :])
        nc.scalar.activation(bent[:, 2, :], diff[:, 2, :], ACT.Tanh)
        differ(3, lows[:, 2, :])
        w1_first = quantize(w1_woven[:, halves(0), :], "w1_first")
        for c in range(2):
            nc.scalar.activation(bent[:, 3, halves(c)], diff[:, 3, halves(c)], ACT.Tanh)
        nc.scalar.activation(diff[:, 3, H - 1 : H], d_sb[0][:, 0:1], ACT.Abs_reciprocal_sqrt, bias=0.5, scale=0.0)

        def quarter(u):
            return slice(u * P, (u + 1) * P)

        def mix(u):
            zu = sb([P, P, PACK], BF16, "z%d" % u)
            nc.vector.tensor_tensor(
                zu[:].rearrange("p (a i) t -> p a t i", i=4),
                yg[:, :, quarter(u)].rearrange("p t (a i) -> p a t i", i=4),
                bent[:, :, quarter(u)].rearrange("p t (a i) -> p a t i", i=4),
                ALU.mult,
            )
            return zu[:]

        z = [mix(0)]
        z_q = []
        for u in range(PACK):
            if u + 1 < PACK:
                z.append(mix(u + 1))
            z_q.append(quantize(z[u], "z%d" % u))
        w1_second = quantize(w1_woven[:, halves(1), :], "w1_second", tag="z0")

        pair = [psum.tile([P, 2, P], F32, name="bank%d" % u) for u in range(PACK)]
        whole = [psum.tile([P, H], F32, name="bank%d" % (PACK + e)) for e in range(2)]
        size = sb([P, 2, H], F32, "size")
        root = sb([P, PACK, H], F32, "root")
        inv = [sb([P, H], F32, "inv%d" % t) for t in range(PACK)]

        def invert_root(u):
            nc.scalar.activation(root[:, 0:2, quarter(u)], size[:, :, quarter(u)], ACT.Abs_reciprocal_sqrt, bias=0.5)

        for u in range(PACK):
            for t in range(2):
                product(pair[u][:, t, :], w1_first, t, z_q[u])
            nc.scalar.activation(size[:, :, quarter(u)], pair[u][:], ACT.Abs)
            if u > 0:
                invert_root(u - 1)
        invert_root(PACK - 1)
        for e in range(2):
            for u in range(PACK):
                product(whole[e][:, quarter(u)], w1_second, e, z_q[u])
        for cols in (halves(0), quarter(2)):
            for t in range(2):
                nc.vector.tensor_tensor(inv[t][:, cols], root[:, t, cols], root[:, t, cols], ALU.mult)
        for t in range(2):
            nc.scalar.activation(inv[t][:, quarter(3)], root[:, t, quarter(3)], ACT.Square)
        flat = [w[:] for w in whole]
        for u in range(2):
            nc.scalar.activation(size[:, u, :], flat[u], ACT.Abs)
        h_sb = [root[:, u, :] for u in range(2)]
        for u in range(2):
            nc.scalar.activation(root[:, 2 + u, :], size[:, u, :], ACT.Abs_reciprocal_sqrt, bias=0.5)
            nc.scalar.copy(h_sb[u], flat[u])
            nc.scalar.activation(inv[2 + u][:], root[:, 2 + u, :], ACT.Square)

        rows = out.rearrange("(p t) n -> p t n", t=PACK)
        for t in range(PACK):
            res = sb([P, H], F32, "res%d" % t)
            if t < 2:
                got = sb([P, H], F32, "got%d" % t)
                for c in range(2):
                    nc.vector.tensor_copy(got[:, halves(c)], inv[t][:].indirect(entries(n3_l, c)))
                for u in range(PACK):
                    nc.vector.tensor_tensor(res[:, quarter(u)], got[:, quarter(u)], pair[u][:, t, :], ALU.mult)
            else:
                for c in range(2):
                    nc.vector.tensor_tensor(
                        res[:, halves(c)], inv[t][:].indirect(entries(n3_l, c)), h_sb[t - 2][:, halves(c)], ALU.mult
                    )
                    if t == PACK - 1:
                        nc.sync.dma_start(rows[:, t, halves(c)], res[:, halves(c)])
            if t < PACK - 1:
                nc.sync.dma_start(rows[:, t, :], res[:])
